import numpy as np
import ml_dtypes


def mxq(x, axis, fmt="e4m3"):
    dtype, down = {"e4m3": (ml_dtypes.float8_e4m3fn, 7), "e5m2": (ml_dtypes.float8_e5m2, 14)}[fmt]
    v = np.moveaxis(np.asarray(x, np.float32).astype(ml_dtypes.bfloat16).astype(np.float64), axis, -1)
    blocks = v.reshape(v.shape[:-1] + (-1, 32))
    amax = np.abs(blocks).max(-1, keepdims=True)
    byte = np.maximum(np.where(amax > 0, np.frexp(amax)[1] - 1 + 127, 0) - down, 1)
    scale = np.exp2(byte - 127.0)
    codes = (blocks / scale).astype(np.float32).astype(dtype).astype(np.float64)
    return np.moveaxis((codes * scale).reshape(v.shape), -1, axis)


WIDE = False


def mx_kscale(k):
    if not WIDE:
        return np.ones(k)
    levels = np.array([10, -10, 5, -5, 0])
    if k % 512:
        return np.exp2(np.random.permutation(np.resize(levels, k // 32))).repeat(32)
    a = np.empty((k // 512, 16))
    for p in range(k // 512):
        a[p, :8] = np.random.permutation(np.resize(levels, 8))
        for g in range(8):
            far = levels[np.abs(levels - a[p, g]) >= 10]
            a[p, g + 8] = far[np.random.randint(len(far))]
    return np.exp2(a.ravel()).repeat(32)


def f64(x):
    return np.asarray(x).astype(np.float64)


def striped(idx):
    return np.tile(idx.reshape(-1, 16).T, (8, 1)).astype(np.uint16)


def unstriped(offs):
    return offs[:16].T.reshape(-1).astype(np.int64)


def pack_weight(w):
    k, n = w.shape
    w = f64(np.asarray(w, np.float32).astype(ml_dtypes.bfloat16)).reshape(k // 32, 32, n)
    amax = np.abs(w).max(1)
    byte = np.clip(np.where(amax > 0, np.frexp(amax)[1] - 1 + 127 - 7, 1), 1, 254)
    scaled = (w * np.exp2(127.0 - byte)[:, None, :]).reshape(k, n).astype(np.float32)
    words = np.ascontiguousarray(scaled.reshape(k // 512, 128, 4, n).transpose(0, 1, 3, 2)).astype(ml_dtypes.float8_e4m3fn).view(np.uint8)
    return words, np.ascontiguousarray(byte.astype(np.uint8).reshape(k // 512, 16, n))


def unpack_weight(words, scales):
    g, p, n, _ = words.shape
    vals = np.ascontiguousarray(words).view(ml_dtypes.float8_e4m3fn).astype(np.float64) * np.repeat(np.exp2(scales.astype(np.float64) - 127.0), 8, axis=1)[..., None]
    return vals.transpose(0, 1, 3, 2).reshape(g * 512, n)


def planes(y):
    n, m = y.shape
    v = y.astype(np.float32).astype(ml_dtypes.bfloat16).astype(np.float64).reshape(n // 32, 32, m)
    top = np.abs(v).max(1)
    byte = np.clip(np.where(top > 0, np.frexp(top)[1] - 1 + 127 - 7, 1), 1, 254)
    codes = (v * np.exp2(127.0 - byte)[:, None, :]).reshape(n, m).astype(np.float32).astype(ml_dtypes.float8_e4m3fn).view(np.uint8)
    words = codes.reshape(n // 512, 128, 4, m).transpose(0, 1, 3, 2)
    return np.ascontiguousarray(words), np.ascontiguousarray(byte.astype(np.uint8).reshape(n // 512, 16, m))


def silu(v):
    return v / (1.0 + np.exp(-np.maximum(v, -700.0)))


K, T, S, N = 512, 1024, 512, 512
P = 2 ** 7


def setup_inputs():
    n = np.random.standard_normal
    s = mx_kscale(K)[:, None]
    packed_xT = pack_weight(n((K, T)) * s)
    return {
        "x_words": packed_xT[0],
        "x_scales": packed_xT[1],
        "w1": (n((K, N)) / np.sqrt(K) / s).astype(np.float32),
        "gain": (np.tile(np.random.uniform(0.5, 1.5, T), (P, 1))).astype(np.float32),
        "shift": (np.tile(0.5 * np.random.standard_normal(T), (P, 1))).astype(np.float32),
        "wsum": (n((N, 1))).astype(np.float32),
        "offs": striped(np.random.permutation(T)[:S]),
    }


def reference(x_words, x_scales, w1, gain, shift, wsum, offs):
    xq = unpack_weight(x_words, x_scales)[:, unstriped(offs)]
    y = mxq(f64(w1), 0, "e4m3").T @ xq
    g = f64(gain)[:1][:, unstriped(offs)]
    t = f64(shift)[:1][:, unstriped(offs)]
    out_0 = silu(y * g + f64(wsum) * t)
    return (out_0,) + planes(out_0)

@@ -1,0 +1,167 @@
+from contextlib import ExitStack
+
+import concourse.mybir as mybir
+from concourse.masks import make_identity
+
+K, T, S, N = 512, 1024, 512, 512
+FLOPS = 2 * K * S * N
+
+F32 = mybir.dt.float32
+BF16 = mybir.dt.bfloat16
+I32 = mybir.dt.int32
+U32 = mybir.dt.uint32
+U16 = mybir.dt.uint16
+U8 = mybir.dt.uint8
+FP8X4 = mybir.dt.float8_e4m3fn_x4
+MULT = mybir.AluOpType.mult
+ADD = mybir.AluOpType.add
+SILU = mybir.ActivationFunctionType.Silu
+COPY = mybir.ActivationFunctionType.Copy
+
+P = 128
+PACK = 4
+CHUNKS = S // P
+LIST_COLS = P // 16
+HALF = N // 2
+
+
+def interleave_views(dst, src):
+    return (
+        dst.rearrange("p (c i) t -> p c t i", i=4),
+        src.rearrange("p t (c i) -> p c t i", i=4),
+    )
+
+
+def tile_picked_zdq_linsilu_po_kernel(
+    tc, x_words, x_scales, w1, gain, shift, wsum, offs, out_0, out_1, out_2
+):
+    nc = tc.nc
+    with ExitStack() as ctx:
+        keep = ctx.enter_context(tc.tile_pool(name="keep", bufs=1))
+        once = ctx.enter_context(tc.psum_pool(name="once", bufs=1))
+        ring = ctx.enter_context(tc.psum_pool(name="ring", bufs=3))
+
+        offsets = keep.tile([P, S // 16], U16, name="offsets")
+        nc.sync.dma_start(offsets[:], offs)
+
+        row_table = keep.tile([P, T], F32, name="row_table")
+        nc.sync.dma_start(out=row_table[0:16, :], in_=gain[0:16, :])
+        nc.sync.dma_start(out=row_table[16:32, :], in_=shift[0:16, :])
+
+        byte_table = keep.tile([P, T], U8, name="byte_table")
+        nc.vector.memset(byte_table[:].bitcast(I32), 0)
+        warm = keep.tile([P, 8], F32, name="warm")
+        nc.vector.memset(warm[:], 0.0)
+        nc.scalar.activation(out=warm[:, 4:5], in_=warm[:, 0:1], func=SILU)
+        nc.vector.memset(row_table[32:64, :], 0.0)
+        nc.vector.memset(row_table[64:128, :], 0.0)
+
+        w_view = w1.rearrange("(p j) c -> p j c", j=PACK)
+        w_raw = [keep.tile([P, PACK, HALF], F32, name=f"w_raw{h}") for h in range(2)]
+        for h in range(2):
+            nc.sync.dma_start(out=w_raw[h][:], in_=w_view[:, :, h * HALF : (h + 1) * HALF])
+        for q in range(4):
+            nc.sync.dma_start(
+                out=byte_table[32 * q : 32 * q + 4, :].bitcast(I32),
+                in_=x_scales[0, 4 * q : 4 * q + 4, :].bitcast(I32),
+            )
+        word_table = keep.tile([P, T], U32, name="word_table")
+        nc.sync.dma_start(
+            out=word_table[:].bitcast(I32), in_=x_words[0].rearrange("p n t -> p (n t)").bitcast(I32)
+        )
+        wsum_cols = keep.tile([P, PACK], F32, name="wsum_cols")
+        nc.sync.dma_start(out=wsum_cols[:], in_=wsum.rearrange("(p t) o -> p (t o)", t=PACK))
+
+        ident = keep.tile([P, P], F32, name="ident")
+        make_identity(nc, ident[:])
+
+        rows = keep.tile([P, S], F32, name="rows")
+        nc.vector.tensor_copy(out=rows[:], in_=row_table[:].indirect(offsets[:]))
+        x_bytes = keep.tile([P, S], U8, name="x_bytes", align_bytes=64)
+        nc.vector.tensor_copy(out=x_bytes[:], in_=byte_table[:].indirect(offsets[:]))
+
+        wsum_rows = once.tile([P, PACK, P], F32, name="wsum_rows")
+        for t in range(PACK):
+            nc.tensor.transpose(wsum_rows[:, t, :], wsum_cols[:, t : t + 1].to_broadcast([P, P]), ident[:])
+        turned = once.tile([P, CHUNKS, P], F32, name="turned")
+        for c in range(CHUNKS):
+            nc.tensor.transpose(turned[:, c, :], rows[:, c * P : (c + 1) * P], ident[:])
+        factors = keep.tile([P, CHUNKS, 2], F32, name="factors")
+        nc.scalar.copy(out=factors[:], in_=turned[:, :, 0:32:16])
+
+        w_codes = keep.tile([P, N], U32, name="w_codes", align_bytes=64)
+        w_bytes = keep.tile([P, N], U8, name="w_bytes", align_bytes=64)
+        for h in range(2):
+            w_bf = keep.tile([P, HALF, PACK], BF16, name=f"w_bf{h}", align_bytes=64)
+            dst, src = interleave_views(w_bf[:], w_raw[h][:])
+            nc.scalar.copy(out=dst, in_=src)
+            cols = slice(h * HALF, (h + 1) * HALF)
+            nc.vector.quantize_mx(
+                out=w_codes[:, cols].bitcast(FP8X4),
+                scales=w_bytes[:, cols],
+                in_=w_bf[:].rearrange("p c j -> p (c j)"),
+            )
+
+        x_codes = []
+        for c in range(CHUNKS):
+            codes = keep.tile([P, P], U32, name=f"x_codes{c}", align_bytes=64)
+            nc.vector.tensor_copy(
+                out=codes[:], in_=word_table[:].indirect(offsets[:, c * LIST_COLS : (c + 1) * LIST_COLS])
+            )
+            x_codes.append(codes)
+
+        out_view = out_0.rearrange("(p t) j -> p t j", t=PACK)
+        code_view = out_1[0].rearrange("p n t -> p (n t)").bitcast(I32)
+        out_codes = keep.tile([P, S], U32, name="out_codes", align_bytes=64)
+        out_bytes = keep.tile([P, S], U8, name="out_bytes", align_bytes=64)
+        for c in range(CHUNKS):
+            cols = slice(c * P, (c + 1) * P)
+            offset_term = keep.tile([P, N], F32, name=f"offset_term{c}")
+            nc.scalar.activation(
+                out=offset_term[:],
+                in_=wsum_rows[:].rearrange("p t m -> p (t m)"),
+                func=COPY,
+                scale=factors[:, c, 1:2],
+            )
+            acc = ring.tile([P, N], F32, name="acc")
+            nc.tensor.matmul_mx(
+                out=acc[:],
+                lhsT=x_codes[c][:].bitcast(FP8X4),
+                lhsT_scale=x_bytes[:, cols],
+                rhs=w_codes[:].bitcast(FP8X4),
+                rhs_scale=w_bytes[:],
+                start=True,
+                stop=True,
+            )
+            pre = keep.tile([P, PACK, P], F32, name=f"pre{c}")
+            nc.vector.scalar_tensor_tensor(
+                out=pre[:],
+                in0=acc[:].rearrange("p (m t) -> p t m", t=PACK),
+                scalar=factors[:, c, 0:1],
+                in1=offset_term[:].rearrange("p (t m) -> p t m", t=PACK),
+                op0=MULT,
+                op1=ADD,
+            )
+            back = ring.tile([P, PACK, P], F32, name="back")
+            for t in range(PACK):
+                nc.tensor.transpose(back[:, t, :], pre[:, t, :], ident[:])
+            result = keep.tile([P, PACK, P], F32, name=f"result{c}")
+            nc.scalar.activation(out=result[:], in_=back[:], func=SILU)
+            nc.sync.dma_start(out=out_view[:, :, cols], in_=result[:])
+            rounded = keep.tile([P, P, PACK], BF16, name=f"rounded{c}", align_bytes=64)
+            dst, src = interleave_views(rounded[:], result[:])
+            nc.vector.tensor_copy(out=dst, in_=src)
+            nc.vector.quantize_mx(
+                out=out_codes[:, cols].bitcast(FP8X4),
+                scales=out_bytes[:, cols],
+                in_=rounded[:].rearrange("p j t -> p (j t)"),
+            )
+            if c % 2 == 1:
+                pair = slice((c - 1) * P, (c + 1) * P)
+                nc.sync.dma_start(out=code_view[:, pair], in_=out_codes[:, pair].bitcast(I32))
+        for q in range(4):
+            queue = nc.scalar if q % 2 else nc.sync
+            queue.dma_start(
+                out=out_2[0, 4 * q : 4 * q + 4, :].bitcast(I32),
+                in_=out_bytes[32 * q : 32 * q + 4, :].bitcast(I32),
+            )

@@ -23,6 +23,7 @@ PACK = 4
 CHUNKS = S // P
 LIST_COLS = P // 16
 HALF = N // 2
+SCALAR_SHARE = 160
 
 
 def interleave_views(dst, src):
@@ -38,129 +39,161 @@ def tile_picked_zdq_linsilu_po_kernel(
     nc = tc.nc
     with ExitStack() as ctx:
         keep = ctx.enter_context(tc.tile_pool(name="keep", bufs=1))
-        once = ctx.enter_context(tc.psum_pool(name="once", bufs=1))
-        ring = ctx.enter_context(tc.psum_pool(name="ring", bufs=3))
+        psum = ctx.enter_context(tc.psum_pool(name="psum", bufs=1))
 
         offsets = keep.tile([P, S // 16], U16, name="offsets")
         nc.sync.dma_start(offsets[:], offs)
-
-        row_table = keep.tile([P, T], F32, name="row_table")
-        nc.sync.dma_start(out=row_table[0:16, :], in_=gain[0:16, :])
-        nc.sync.dma_start(out=row_table[16:32, :], in_=shift[0:16, :])
-
         byte_table = keep.tile([P, T], U8, name="byte_table")
-        nc.vector.memset(byte_table[:].bitcast(I32), 0)
-        warm = keep.tile([P, 8], F32, name="warm")
-        nc.vector.memset(warm[:], 0.0)
-        nc.scalar.activation(out=warm[:, 4:5], in_=warm[:, 0:1], func=SILU)
-        nc.vector.memset(row_table[32:64, :], 0.0)
-        nc.vector.memset(row_table[64:128, :], 0.0)
-
-        w_view = w1.rearrange("(p j) c -> p j c", j=PACK)
-        w_raw = [keep.tile([P, PACK, HALF], F32, name=f"w_raw{h}") for h in range(2)]
-        for h in range(2):
-            nc.sync.dma_start(out=w_raw[h][:], in_=w_view[:, :, h * HALF : (h + 1) * HALF])
+        nc.gpsimd.memset(byte_table[:].bitcast(I32), 0)
+        row_table = keep.tile([P, T], F32, name="row_table")
+        nc.scalar.dma_start(out=row_table[0:16, :], in_=gain[0:16, :])
+        nc.scalar.dma_start(out=row_table[16:32, :], in_=shift[0:16, :])
         for q in range(4):
-            nc.sync.dma_start(
+            queue = nc.scalar if q == 3 else nc.sync
+            queue.dma_start(
                 out=byte_table[32 * q : 32 * q + 4, :].bitcast(I32),
                 in_=x_scales[0, 4 * q : 4 * q + 4, :].bitcast(I32),
             )
+
+        ident = keep.tile([P, P], F32, name="ident")
+        nc.vector.memset(ident[:], 0.0)
+        make_identity(nc, ident[:], nomemset=True)
+        warm = keep.tile([P, 8], F32, name="warm")
+        nc.vector.memset(warm[:], 0.0)
+        nc.scalar.activation(out=warm[:, 4:5], in_=warm[:, 0:1], func=SILU)
+        nc.vector.memset(row_table[32:64, :].bitcast(I32), 0)
+        nc.vector.memset(row_table[64:128, :].bitcast(I32), 0)
+
+        w_view = w1.rearrange("(p j) c -> p j c", j=PACK)
+        w_raw = [keep.tile([P, PACK, HALF], F32, name=f"w_raw{h}", tag=f"w_raw{h}") for h in range(2)]
+        for h in range(2):
+            nc.sync.dma_start(out=w_raw[h][:], in_=w_view[:, :, h * HALF : (h + 1) * HALF])
+        wsum_cols = keep.tile([P, PACK], F32, name="wsum_cols")
+        nc.sync.dma_start(out=wsum_cols[:], in_=wsum.rearrange("(p t) o -> p (t o)", t=PACK))
         word_table = keep.tile([P, T], U32, name="word_table")
         nc.sync.dma_start(
             out=word_table[:].bitcast(I32), in_=x_words[0].rearrange("p n t -> p (n t)").bitcast(I32)
         )
-        wsum_cols = keep.tile([P, PACK], F32, name="wsum_cols")
-        nc.sync.dma_start(out=wsum_cols[:], in_=wsum.rearrange("(p t) o -> p (t o)", t=PACK))
 
-        ident = keep.tile([P, P], F32, name="ident")
-        make_identity(nc, ident[:])
-
-        rows = keep.tile([P, S], F32, name="rows")
+        rows = keep.tile([P, S], F32, name="rows", tag="rows", align_bytes=64)
         nc.vector.tensor_copy(out=rows[:], in_=row_table[:].indirect(offsets[:]))
         x_bytes = keep.tile([P, S], U8, name="x_bytes", align_bytes=64)
         nc.vector.tensor_copy(out=x_bytes[:], in_=byte_table[:].indirect(offsets[:]))
 
-        wsum_rows = once.tile([P, PACK, P], F32, name="wsum_rows")
-        for t in range(PACK):
-            nc.tensor.transpose(wsum_rows[:, t, :], wsum_cols[:, t : t + 1].to_broadcast([P, P]), ident[:])
-        turned = once.tile([P, CHUNKS, P], F32, name="turned")
+        turned = psum.tile([P, CHUNKS, P], F32, name="turned", tag="turned")
         for c in range(CHUNKS):
             nc.tensor.transpose(turned[:, c, :], rows[:, c * P : (c + 1) * P], ident[:])
-        factors = keep.tile([P, CHUNKS, 2], F32, name="factors")
-        nc.scalar.copy(out=factors[:], in_=turned[:, :, 0:32:16])
+        wsum_rows = psum.tile([P, PACK, P], F32, name="wsum_rows")
+        for t in range(PACK):
+            nc.tensor.transpose(wsum_rows[:, t, :], wsum_cols[:, t : t + 1].to_broadcast([P, P]), ident[:])
 
         w_codes = keep.tile([P, N], U32, name="w_codes", align_bytes=64)
         w_bytes = keep.tile([P, N], U8, name="w_bytes", align_bytes=64)
-        for h in range(2):
-            w_bf = keep.tile([P, HALF, PACK], BF16, name=f"w_bf{h}", align_bytes=64)
-            dst, src = interleave_views(w_bf[:], w_raw[h][:])
-            nc.scalar.copy(out=dst, in_=src)
+        w_bf = [keep.tile([P, HALF, PACK], BF16, name=f"w_bf{h}", align_bytes=64) for h in range(2)]
+        x_codes = keep.tile([P, S], U32, name="x_codes", tag="rows", align_bytes=64)
+        acc_tags = ["acc0", "acc1", "acc2", "acc0"]
+
+        def round_weights(copy, h, cols):
+            dst, src = interleave_views(w_bf[h][:, cols, :], w_raw[h][:, :, cols])
+            copy(out=dst, in_=src)
+
+        def quantize_weights(h):
             cols = slice(h * HALF, (h + 1) * HALF)
             nc.vector.quantize_mx(
                 out=w_codes[:, cols].bitcast(FP8X4),
                 scales=w_bytes[:, cols],
-                in_=w_bf[:].rearrange("p c j -> p (c j)"),
+                in_=w_bf[h][:].rearrange("p c j -> p (c j)"),
             )
 
-        x_codes = []
-        for c in range(CHUNKS):
-            codes = keep.tile([P, P], U32, name=f"x_codes{c}", align_bytes=64)
-            nc.vector.tensor_copy(
-                out=codes[:], in_=word_table[:].indirect(offsets[:, c * LIST_COLS : (c + 1) * LIST_COLS])
-            )
-            x_codes.append(codes)
-
-        out_view = out_0.rearrange("(p t) j -> p t j", t=PACK)
-        code_view = out_1[0].rearrange("p n t -> p (n t)").bitcast(I32)
-        out_codes = keep.tile([P, S], U32, name="out_codes", align_bytes=64)
-        out_bytes = keep.tile([P, S], U8, name="out_bytes", align_bytes=64)
-        for c in range(CHUNKS):
+        def multiply(acc, c):
             cols = slice(c * P, (c + 1) * P)
-            offset_term = keep.tile([P, N], F32, name=f"offset_term{c}")
-            nc.scalar.activation(
-                out=offset_term[:],
-                in_=wsum_rows[:].rearrange("p t m -> p (t m)"),
-                func=COPY,
-                scale=factors[:, c, 1:2],
-            )
-            acc = ring.tile([P, N], F32, name="acc")
             nc.tensor.matmul_mx(
                 out=acc[:],
-                lhsT=x_codes[c][:].bitcast(FP8X4),
+                lhsT=x_codes[:, cols].bitcast(FP8X4),
                 lhsT_scale=x_bytes[:, cols],
                 rhs=w_codes[:].bitcast(FP8X4),
                 rhs_scale=w_bytes[:],
                 start=True,
                 stop=True,
             )
+
+        def make_offset_term(out, c):
+            nc.scalar.activation(
+                out=out,
+                in_=wsum_rows[:].rearrange("p t m -> p (t m)"),
+                func=COPY,
+                scale=factors[:, c, 1:2],
+            )
+
+        round_weights(nc.scalar.copy, 0, slice(0, HALF))
+        quantize_weights(0)
+        factors = keep.tile([P, CHUNKS, 2], F32, name="factors", tag="w_raw0")
+        nc.scalar.copy(out=factors[:], in_=turned[:, :, 0:32:16])
+        round_weights(nc.scalar.copy, 1, slice(0, SCALAR_SHARE))
+        round_weights(nc.vector.tensor_copy, 1, slice(SCALAR_SHARE, HALF))
+        quantize_weights(1)
+        for first, last in ((0, 1), (1, 2), (2, 4)):
+            nc.vector.tensor_copy(
+                out=x_codes[:, first * P : last * P],
+                in_=word_table[:].indirect(offsets[:, first * LIST_COLS : last * LIST_COLS]),
+            )
+        terms = keep.tile([P, CHUNKS, N], F32, name="terms", tag="w_raw1")
+        offset_term = [terms[:, c, :] for c in range(CHUNKS)]
+        for c in range(CHUNKS):
+            make_offset_term(offset_term[c], c)
+
+        out_view = out_0.rearrange("(p t) j -> p t j", t=PACK)
+        code_view = out_1[0].rearrange("p n t -> p (n t)").bitcast(I32)
+        out_codes = keep.tile([P, S], U32, name="out_codes", align_bytes=64)
+        out_bytes = keep.tile([P, S], U8, name="out_bytes", align_bytes=64)
+        back_tags = ["back0", "back1", "back2", "turned"]
+        results = []
+        for c in range(CHUNKS):
+            cols = slice(c * P, (c + 1) * P)
+            acc = psum.tile([P, N], F32, name=f"acc{c}", tag=acc_tags[c])
+            multiply(acc, c)
             pre = keep.tile([P, PACK, P], F32, name=f"pre{c}")
             nc.vector.scalar_tensor_tensor(
                 out=pre[:],
                 in0=acc[:].rearrange("p (m t) -> p t m", t=PACK),
                 scalar=factors[:, c, 0:1],
-                in1=offset_term[:].rearrange("p (t m) -> p t m", t=PACK),
+                in1=offset_term[c].rearrange("p (t m) -> p t m", t=PACK),
                 op0=MULT,
                 op1=ADD,
             )
-            back = ring.tile([P, PACK, P], F32, name="back")
+            back = psum.tile([P, PACK, P], F32, name=f"back{c}", tag=back_tags[c])
             for t in range(PACK):
                 nc.tensor.transpose(back[:, t, :], pre[:, t, :], ident[:])
             result = keep.tile([P, PACK, P], F32, name=f"result{c}")
             nc.scalar.activation(out=result[:], in_=back[:], func=SILU)
             nc.sync.dma_start(out=out_view[:, :, cols], in_=result[:])
-            rounded = keep.tile([P, P, PACK], BF16, name=f"rounded{c}", align_bytes=64)
-            dst, src = interleave_views(rounded[:], result[:])
+            results.append(result)
+
+        rounded = [keep.tile([P, P, PACK], BF16, name=f"rounded{c}", align_bytes=64) for c in range(CHUNKS)]
+
+        def round_result(c):
+            dst, src = interleave_views(rounded[c][:], results[c][:])
             nc.vector.tensor_copy(out=dst, in_=src)
+
+        def quantize_result(c):
+            cols = slice(c * P, (c + 1) * P)
             nc.vector.quantize_mx(
                 out=out_codes[:, cols].bitcast(FP8X4),
                 scales=out_bytes[:, cols],
-                in_=rounded[:].rearrange("p j t -> p (j t)"),
+                in_=rounded[c][:].rearrange("p j t -> p (j t)"),
             )
-            if c % 2 == 1:
-                pair = slice((c - 1) * P, (c + 1) * P)
-                nc.sync.dma_start(out=code_view[:, pair], in_=out_codes[:, pair].bitcast(I32))
+
+        round_result(0)
+        for c in range(1, CHUNKS):
+            round_result(c)
+            quantize_result(c - 1)
+        early = slice(0, S - P)
+        nc.sync.dma_start(out=code_view[:, early], in_=out_codes[:, early].bitcast(I32))
+        quantize_result(CHUNKS - 1)
+        late = slice(S - P, S)
+        nc.scalar.dma_start(out=code_view[:, late], in_=out_codes[:, late].bitcast(I32))
         for q in range(4):
-            queue = nc.scalar if q % 2 else nc.sync
+            queue = nc.scalar if q == 3 else nc.sync
             queue.dma_start(
                 out=out_2[0, 4 * q : 4 * q + 4, :].bitcast(I32),
                 in_=out_bytes[32 * q : 32 * q + 4, :].bitcast(I32),

@@ -20,9 +20,12 @@ COPY = mybir.ActivationFunctionType.Copy
 
 P = 128
 PACK = 4
+QUADS = 4
 CHUNKS = S // P
-LIST_COLS = P // 16
+LIST_ROWS = 16
+LIST_COLS = P // LIST_ROWS
 HALF = N // 2
+TABLE_ROWS = 16
 SCALAR_SHARE = 160
 
 
@@ -41,15 +44,16 @@ def tile_picked_zdq_linsilu_po_kernel(
         keep = ctx.enter_context(tc.tile_pool(name="keep", bufs=1))
         psum = ctx.enter_context(tc.psum_pool(name="psum", bufs=1))
 
-        offsets = keep.tile([P, S // 16], U16, name="offsets")
+        offsets = keep.tile([P, S // LIST_ROWS], U16, name="offsets")
         nc.sync.dma_start(offsets[:], offs)
+
         byte_table = keep.tile([P, T], U8, name="byte_table")
         nc.gpsimd.memset(byte_table[:].bitcast(I32), 0)
         row_table = keep.tile([P, T], F32, name="row_table")
-        nc.scalar.dma_start(out=row_table[0:16, :], in_=gain[0:16, :])
-        nc.scalar.dma_start(out=row_table[16:32, :], in_=shift[0:16, :])
-        for q in range(4):
-            queue = nc.scalar if q == 3 else nc.sync
+        nc.scalar.dma_start(out=row_table[0:TABLE_ROWS, :], in_=gain[0:TABLE_ROWS, :])
+        nc.scalar.dma_start(out=row_table[TABLE_ROWS : 2 * TABLE_ROWS, :], in_=shift[0:TABLE_ROWS, :])
+        for q in range(QUADS):
+            queue = nc.scalar if q == QUADS - 1 else nc.sync
             queue.dma_start(
                 out=byte_table[32 * q : 32 * q + 4, :].bitcast(I32),
                 in_=x_scales[0, 4 * q : 4 * q + 4, :].bitcast(I32),
@@ -91,7 +95,6 @@ def tile_picked_zdq_linsilu_po_kernel(
         w_bytes = keep.tile([P, N], U8, name="w_bytes", align_bytes=64)
         w_bf = [keep.tile([P, HALF, PACK], BF16, name=f"w_bf{h}", align_bytes=64) for h in range(2)]
         x_codes = keep.tile([P, S], U32, name="x_codes", tag="rows", align_bytes=64)
-        acc_tags = ["acc0", "acc1", "acc2", "acc0"]
 
         def round_weights(copy, h, cols):
             dst, src = interleave_views(w_bf[h][:, cols, :], w_raw[h][:, :, cols])
@@ -105,8 +108,38 @@ def tile_picked_zdq_linsilu_po_kernel(
                 in_=w_bf[h][:].rearrange("p c j -> p (c j)"),
             )
 
-        def multiply(acc, c):
+        round_weights(nc.scalar.copy, 0, slice(0, HALF))
+        quantize_weights(0)
+        factors = keep.tile([P, CHUNKS, 2], F32, name="factors", tag="w_raw0")
+        nc.scalar.copy(out=factors[:], in_=turned[:, :, 0 : 2 * TABLE_ROWS : TABLE_ROWS])
+        round_weights(nc.scalar.copy, 1, slice(0, SCALAR_SHARE))
+        round_weights(nc.vector.tensor_copy, 1, slice(SCALAR_SHARE, HALF))
+        quantize_weights(1)
+
+        for first, last in ((0, 1), (1, 2), (2, CHUNKS)):
+            nc.vector.tensor_copy(
+                out=x_codes[:, first * P : last * P],
+                in_=word_table[:].indirect(offsets[:, first * LIST_COLS : last * LIST_COLS]),
+            )
+
+        terms = keep.tile([P, CHUNKS, N], F32, name="terms", tag="w_raw1")
+        for c in range(CHUNKS):
+            nc.scalar.activation(
+                out=terms[:, c, :],
+                in_=wsum_rows[:].rearrange("p t m -> p (t m)"),
+                func=COPY,
+                scale=factors[:, c, 1:2],
+            )
+
+        out_view = out_0.rearrange("(p t) j -> p t j", t=PACK)
+        code_view = out_1[0].rearrange("p n t -> p (n t)").bitcast(I32)
+        out_codes = keep.tile([P, S], U32, name="out_codes", align_bytes=64)
+        out_bytes = keep.tile([P, S], U8, name="out_bytes", align_bytes=64)
+        back_tags = ["back0", "back1", "turned", "acc0"]
+        results = []
+        for c in range(CHUNKS):
             cols = slice(c * P, (c + 1) * P)
+            acc = psum.tile([P, N], F32, name=f"acc{c}", tag=f"acc{c}")
             nc.tensor.matmul_mx(
                 out=acc[:],
                 lhsT=x_codes[:, cols].bitcast(FP8X4),
@@ -116,48 +149,12 @@ def tile_picked_zdq_linsilu_po_kernel(
                 start=True,
                 stop=True,
             )
-
-        def make_offset_term(out, c):
-            nc.scalar.activation(
-                out=out,
-                in_=wsum_rows[:].rearrange("p t m -> p (t m)"),
-                func=COPY,
-                scale=factors[:, c, 1:2],
-            )
-
-        round_weights(nc.scalar.copy, 0, slice(0, HALF))
-        quantize_weights(0)
-        factors = keep.tile([P, CHUNKS, 2], F32, name="factors", tag="w_raw0")
-        nc.scalar.copy(out=factors[:], in_=turned[:, :, 0:32:16])
-        round_weights(nc.scalar.copy, 1, slice(0, SCALAR_SHARE))
-        round_weights(nc.vector.tensor_copy, 1, slice(SCALAR_SHARE, HALF))
-        quantize_weights(1)
-        for first, last in ((0, 1), (1, 2), (2, 4)):
-            nc.vector.tensor_copy(
-                out=x_codes[:, first * P : last * P],
-                in_=word_table[:].indirect(offsets[:, first * LIST_COLS : last * LIST_COLS]),
-            )
-        terms = keep.tile([P, CHUNKS, N], F32, name="terms", tag="w_raw1")
-        offset_term = [terms[:, c, :] for c in range(CHUNKS)]
-        for c in range(CHUNKS):
-            make_offset_term(offset_term[c], c)
-
-        out_view = out_0.rearrange("(p t) j -> p t j", t=PACK)
-        code_view = out_1[0].rearrange("p n t -> p (n t)").bitcast(I32)
-        out_codes = keep.tile([P, S], U32, name="out_codes", align_bytes=64)
-        out_bytes = keep.tile([P, S], U8, name="out_bytes", align_bytes=64)
-        back_tags = ["back0", "back1", "back2", "turned"]
-        results = []
-        for c in range(CHUNKS):
-            cols = slice(c * P, (c + 1) * P)
-            acc = psum.tile([P, N], F32, name=f"acc{c}", tag=acc_tags[c])
-            multiply(acc, c)
             pre = keep.tile([P, PACK, P], F32, name=f"pre{c}")
             nc.vector.scalar_tensor_tensor(
                 out=pre[:],
                 in0=acc[:].rearrange("p (m t) -> p t m", t=PACK),
                 scalar=factors[:, c, 0:1],
-                in1=offset_term[c].rearrange("p (t m) -> p t m", t=PACK),
+                in1=terms[:, c, :].rearrange("p (t m) -> p t m", t=PACK),
                 op0=MULT,
                 op1=ADD,
             )
@@ -169,31 +166,28 @@ def tile_picked_zdq_linsilu_po_kernel(
             nc.sync.dma_start(out=out_view[:, :, cols], in_=result[:])
             results.append(result)
 
-        rounded = [keep.tile([P, P, PACK], BF16, name=f"rounded{c}", align_bytes=64) for c in range(CHUNKS)]
+        rounded = [keep.tile([P, 2 * P, PACK], BF16, name=f"rounded{g}", align_bytes=64) for g in range(2)]
 
         def round_result(c):
-            dst, src = interleave_views(rounded[c][:], results[c][:])
+            dst, src = interleave_views(rounded[c // 2][:, (c % 2) * P : (c % 2 + 1) * P, :], results[c][:])
             nc.vector.tensor_copy(out=dst, in_=src)
 
-        def quantize_result(c):
-            cols = slice(c * P, (c + 1) * P)
+        def quantize_pair(g, queue):
+            cols = slice(2 * g * P, 2 * (g + 1) * P)
             nc.vector.quantize_mx(
                 out=out_codes[:, cols].bitcast(FP8X4),
                 scales=out_bytes[:, cols],
-                in_=rounded[c][:].rearrange("p j t -> p (j t)"),
+                in_=rounded[g][:].rearrange("p j t -> p (j t)"),
             )
+            queue.dma_start(out=code_view[:, cols], in_=out_codes[:, cols].bitcast(I32))
 
-        round_result(0)
-        for c in range(1, CHUNKS):
+        for c in range(CHUNKS - 1):
             round_result(c)
-            quantize_result(c - 1)
-        early = slice(0, S - P)
-        nc.sync.dma_start(out=code_view[:, early], in_=out_codes[:, early].bitcast(I32))
-        quantize_result(CHUNKS - 1)
-        late = slice(S - P, S)
-        nc.scalar.dma_start(out=code_view[:, late], in_=out_codes[:, late].bitcast(I32))
-        for q in range(4):
-            queue = nc.scalar if q == 3 else nc.sync
+        quantize_pair(0, nc.sync)
+        round_result(CHUNKS - 1)
+        quantize_pair(1, nc.scalar)
+        for q in range(QUADS):
+            queue = nc.scalar if q == QUADS - 1 else nc.sync
             queue.dma_start(
                 out=out_2[0, 4 * q : 4 * q + 4, :].bitcast(I32),
                 in_=out_bytes[32 * q : 32 * q + 4, :].bitcast(I32),

@@ -25,8 +25,8 @@ CHUNKS = S // P
 LIST_ROWS = 16
 LIST_COLS = P // LIST_ROWS
 HALF = N // 2
-TABLE_ROWS = 16
-SCALAR_SHARE = 160
+SHIFT_ROW = 64
+SCALAR_SHARE = 192
 
 
 def interleave_views(dst, src):
@@ -42,22 +42,24 @@ def tile_picked_zdq_linsilu_po_kernel(
     nc = tc.nc
     with ExitStack() as ctx:
         keep = ctx.enter_context(tc.tile_pool(name="keep", bufs=1))
+        shared = ctx.enter_context(tc.tile_pool(name="shared", bufs=1))
         psum = ctx.enter_context(tc.psum_pool(name="psum", bufs=1))
 
         offsets = keep.tile([P, S // LIST_ROWS], U16, name="offsets")
         nc.sync.dma_start(offsets[:], offs)
 
         byte_table = keep.tile([P, T], U8, name="byte_table")
-        nc.gpsimd.memset(byte_table[:].bitcast(I32), 0)
+        nc.vector.memset(byte_table[:].bitcast(I32), 0)
         row_table = keep.tile([P, T], F32, name="row_table")
-        nc.scalar.dma_start(out=row_table[0:TABLE_ROWS, :], in_=gain[0:TABLE_ROWS, :])
-        nc.scalar.dma_start(out=row_table[TABLE_ROWS : 2 * TABLE_ROWS, :], in_=shift[0:TABLE_ROWS, :])
+        nc.vector.memset(row_table[:].bitcast(I32), 0)
         for q in range(QUADS):
-            queue = nc.scalar if q == QUADS - 1 else nc.sync
+            queue = nc.sync if q < 2 else nc.scalar
             queue.dma_start(
                 out=byte_table[32 * q : 32 * q + 4, :].bitcast(I32),
                 in_=x_scales[0, 4 * q : 4 * q + 4, :].bitcast(I32),
             )
+        nc.sync.dma_start(out=row_table[0:1, :], in_=gain[0:1, :])
+        nc.scalar.dma_start(out=row_table[SHIFT_ROW : SHIFT_ROW + 1, :], in_=shift[0:1, :])
 
         ident = keep.tile([P, P], F32, name="ident")
         nc.vector.memset(ident[:], 0.0)
@@ -65,24 +67,21 @@ def tile_picked_zdq_linsilu_po_kernel(
         warm = keep.tile([P, 8], F32, name="warm")
         nc.vector.memset(warm[:], 0.0)
         nc.scalar.activation(out=warm[:, 4:5], in_=warm[:, 0:1], func=SILU)
-        nc.vector.memset(row_table[32:64, :].bitcast(I32), 0)
-        nc.vector.memset(row_table[64:128, :].bitcast(I32), 0)
 
-        w_view = w1.rearrange("(p j) c -> p j c", j=PACK)
-        w_raw = [keep.tile([P, PACK, HALF], F32, name=f"w_raw{h}", tag=f"w_raw{h}") for h in range(2)]
-        for h in range(2):
-            nc.sync.dma_start(out=w_raw[h][:], in_=w_view[:, :, h * HALF : (h + 1) * HALF])
-        wsum_cols = keep.tile([P, PACK], F32, name="wsum_cols")
-        nc.sync.dma_start(out=wsum_cols[:], in_=wsum.rearrange("(p t) o -> p (t o)", t=PACK))
+        w_raw = keep.tile([P, PACK, N], F32, name="w_raw", tag="w_raw")
+        wsum_cols = shared.tile([P, PACK], F32, name="wsum_cols", offset=0, align_bytes=64)
         word_table = keep.tile([P, T], U32, name="word_table")
+        nc.sync.dma_start(out=w_raw[:], in_=w1.rearrange("(p j) c -> p j c", j=PACK))
+        nc.sync.dma_start(out=wsum_cols[:], in_=wsum.rearrange("(p t) o -> p (t o)", t=PACK))
         nc.sync.dma_start(
             out=word_table[:].bitcast(I32), in_=x_words[0].rearrange("p n t -> p (n t)").bitcast(I32)
         )
 
-        rows = keep.tile([P, S], F32, name="rows", tag="rows", align_bytes=64)
-        nc.vector.tensor_copy(out=rows[:], in_=row_table[:].indirect(offsets[:]))
         x_bytes = keep.tile([P, S], U8, name="x_bytes", align_bytes=64)
         nc.vector.tensor_copy(out=x_bytes[:], in_=byte_table[:].indirect(offsets[:]))
+
+        rows = shared.tile([P, S], F32, name="rows", offset=64, align_bytes=64)
+        nc.vector.tensor_copy(out=rows[:], in_=row_table[:].indirect(offsets[:]))
 
         turned = psum.tile([P, CHUNKS, P], F32, name="turned", tag="turned")
         for c in range(CHUNKS):
@@ -91,38 +90,46 @@ def tile_picked_zdq_linsilu_po_kernel(
         for t in range(PACK):
             nc.tensor.transpose(wsum_rows[:, t, :], wsum_cols[:, t : t + 1].to_broadcast([P, P]), ident[:])
 
+        w_rounded = keep.tile([P, N, PACK], BF16, name="w_rounded", align_bytes=64)
         w_codes = keep.tile([P, N], U32, name="w_codes", align_bytes=64)
         w_bytes = keep.tile([P, N], U8, name="w_bytes", align_bytes=64)
-        w_bf = [keep.tile([P, HALF, PACK], BF16, name=f"w_bf{h}", align_bytes=64) for h in range(2)]
-        x_codes = keep.tile([P, S], U32, name="x_codes", tag="rows", align_bytes=64)
-
-        def round_weights(copy, h, cols):
-            dst, src = interleave_views(w_bf[h][:, cols, :], w_raw[h][:, :, cols])
+        for copy, cols in (
+            (nc.vector.tensor_copy, slice(0, HALF)),
+            (nc.vector.tensor_copy, slice(HALF, N - SCALAR_SHARE)),
+            (nc.scalar.copy, slice(N - SCALAR_SHARE, N)),
+        ):
+            dst, src = interleave_views(w_rounded[:, cols, :], w_raw[:, :, cols])
             copy(out=dst, in_=src)
-
-        def quantize_weights(h):
+        for h in range(2):
             cols = slice(h * HALF, (h + 1) * HALF)
             nc.vector.quantize_mx(
                 out=w_codes[:, cols].bitcast(FP8X4),
                 scales=w_bytes[:, cols],
-                in_=w_bf[h][:].rearrange("p c j -> p (c j)"),
+                in_=w_rounded[:, cols, :].rearrange("p c j -> p (c j)"),
             )
 
-        round_weights(nc.scalar.copy, 0, slice(0, HALF))
-        quantize_weights(0)
-        factors = keep.tile([P, CHUNKS, 2], F32, name="factors", tag="w_raw0")
-        nc.scalar.copy(out=factors[:], in_=turned[:, :, 0 : 2 * TABLE_ROWS : TABLE_ROWS])
-        round_weights(nc.scalar.copy, 1, slice(0, SCALAR_SHARE))
-        round_weights(nc.vector.tensor_copy, 1, slice(SCALAR_SHARE, HALF))
-        quantize_weights(1)
-
-        for first, last in ((0, 1), (1, 2), (2, CHUNKS)):
+        x_codes = shared.tile([P, S], U32, name="x_codes", offset=0, align_bytes=64)
+        accs = [psum.tile([P, N], F32, name=f"acc{c}", tag=f"acc{c}") for c in range(CHUNKS)]
+        for c in range(CHUNKS):
+            cols = slice(c * P, (c + 1) * P)
             nc.vector.tensor_copy(
-                out=x_codes[:, first * P : last * P],
-                in_=word_table[:].indirect(offsets[:, first * LIST_COLS : last * LIST_COLS]),
+                out=x_codes[:, cols],
+                in_=word_table[:].indirect(offsets[:, c * LIST_COLS : (c + 1) * LIST_COLS]),
+            )
+            nc.tensor.matmul_mx(
+                out=accs[c][:],
+                lhsT=x_codes[:, cols].bitcast(FP8X4),
+                lhsT_scale=x_bytes[:, cols],
+                rhs=w_codes[:].bitcast(FP8X4),
+                rhs_scale=w_bytes[:],
+                start=True,
+                stop=True,
             )
 
-        terms = keep.tile([P, CHUNKS, N], F32, name="terms", tag="w_raw1")
+        late = keep.tile([P, CHUNKS * N + 2 * CHUNKS], F32, name="late", tag="w_raw")
+        terms = late[:, 0 : CHUNKS * N].rearrange("p (c m) -> p c m", c=CHUNKS)
+        factors = late[:, CHUNKS * N :].rearrange("p (c f) -> p c f", f=2)
+        nc.scalar.copy(out=factors, in_=turned[:, :, 0:P:SHIFT_ROW])
         for c in range(CHUNKS):
             nc.scalar.activation(
                 out=terms[:, c, :],
@@ -139,20 +146,10 @@ def tile_picked_zdq_linsilu_po_kernel(
         results = []
         for c in range(CHUNKS):
             cols = slice(c * P, (c + 1) * P)
-            acc = psum.tile([P, N], F32, name=f"acc{c}", tag=f"acc{c}")
-            nc.tensor.matmul_mx(
-                out=acc[:],
-                lhsT=x_codes[:, cols].bitcast(FP8X4),
-                lhsT_scale=x_bytes[:, cols],
-                rhs=w_codes[:].bitcast(FP8X4),
-                rhs_scale=w_bytes[:],
-                start=True,
-                stop=True,
-            )
             pre = keep.tile([P, PACK, P], F32, name=f"pre{c}")
             nc.vector.scalar_tensor_tensor(
                 out=pre[:],
-                in0=acc[:].rearrange("p (m t) -> p t m", t=PACK),
+                in0=accs[c][:].rearrange("p (m t) -> p t m", t=PACK),
                 scalar=factors[:, c, 0:1],
                 in1=terms[:, c, :].rearrange("p (t m) -> p t m", t=PACK),
                 op0=MULT,
@@ -166,26 +163,28 @@ def tile_picked_zdq_linsilu_po_kernel(
             nc.sync.dma_start(out=out_view[:, :, cols], in_=result[:])
             results.append(result)
 
-        rounded = [keep.tile([P, 2 * P, PACK], BF16, name=f"rounded{g}", align_bytes=64) for g in range(2)]
+        rounded = keep.tile([P, S, PACK], BF16, name="rounded", align_bytes=64)
 
         def round_result(c):
-            dst, src = interleave_views(rounded[c // 2][:, (c % 2) * P : (c % 2 + 1) * P, :], results[c][:])
+            dst, src = interleave_views(rounded[:, c * P : (c + 1) * P, :], results[c][:])
             nc.vector.tensor_copy(out=dst, in_=src)
 
-        def quantize_pair(g, queue):
-            cols = slice(2 * g * P, 2 * (g + 1) * P)
+        def quantize_result(first, last):
+            cols = slice(first * P, last * P)
             nc.vector.quantize_mx(
                 out=out_codes[:, cols].bitcast(FP8X4),
                 scales=out_bytes[:, cols],
-                in_=rounded[g][:].rearrange("p j t -> p (j t)"),
+                in_=rounded[:, cols, :].rearrange("p j t -> p (j t)"),
             )
-            queue.dma_start(out=code_view[:, cols], in_=out_codes[:, cols].bitcast(I32))
 
         for c in range(CHUNKS - 1):
             round_result(c)
-        quantize_pair(0, nc.sync)
+        quantize_result(0, 2)
+        nc.sync.dma_start(out=code_view[:, 0 : 2 * P], in_=out_codes[:, 0 : 2 * P].bitcast(I32))
         round_result(CHUNKS - 1)
-        quantize_pair(1, nc.scalar)
+        quantize_result(2, 3)
+        quantize_result(3, 4)
+        nc.scalar.dma_start(out=code_view[:, 2 * P : S], in_=out_codes[:, 2 * P : S].bitcast(I32))
         for q in range(QUADS):
             queue = nc.scalar if q == QUADS - 1 else nc.sync
             queue.dma_start(

@@ -108,6 +108,18 @@ def tile_picked_zdq_linsilu_po_kernel(
                 in_=w_rounded[:, cols, :].rearrange("p c j -> p (c j)"),
             )
 
+        unread = psum.tile([P, N], F32, name="unread", tag="back0")
+        for h in range(2):
+            nc.tensor.matmul_mx(
+                out=unread[:, h * HALF : (h + 1) * HALF],
+                lhsT=w_codes[:, 0:P].bitcast(FP8X4),
+                lhsT_scale=w_bytes[:, 0:P],
+                rhs=w_codes[:, 0:HALF].bitcast(FP8X4),
+                rhs_scale=w_bytes[:, 0:HALF],
+                start=True,
+                stop=True,
+            )
+
         x_codes = shared.tile([P, S], U32, name="x_codes", offset=0, align_bytes=64)
         accs = [psum.tile([P, N], F32, name=f"acc{c}", tag=f"acc{c}") for c in range(CHUNKS)]
         for c in range(CHUNKS):

@@ -25,6 +25,7 @@ CHUNKS = S // P
 LIST_ROWS = 16
 LIST_COLS = P // LIST_ROWS
 HALF = N // 2
+EARLY = 1
 SHIFT_ROW = 64
 SCALAR_SHARE = 192
 
@@ -154,10 +155,10 @@ def tile_picked_zdq_linsilu_po_kernel(
         code_view = out_1[0].rearrange("p n t -> p (n t)").bitcast(I32)
         out_codes = keep.tile([P, S], U32, name="out_codes", align_bytes=64)
         out_bytes = keep.tile([P, S], U8, name="out_bytes", align_bytes=64)
+        rounded = keep.tile([P, S, PACK], BF16, name="rounded", align_bytes=64)
         back_tags = ["back0", "back1", "turned", "acc0"]
-        results = []
+        backs, results = [], []
         for c in range(CHUNKS):
-            cols = slice(c * P, (c + 1) * P)
             pre = keep.tile([P, PACK, P], F32, name=f"pre{c}")
             nc.vector.scalar_tensor_tensor(
                 out=pre[:],
@@ -167,19 +168,24 @@ def tile_picked_zdq_linsilu_po_kernel(
                 op0=MULT,
                 op1=ADD,
             )
+            values = pre
+            if c < EARLY:
+                values = keep.tile([P, PACK, P], F32, name=f"values{c}")
+                nc.scalar.activation(out=values[:], in_=pre[:], func=SILU)
             back = psum.tile([P, PACK, P], F32, name=f"back{c}", tag=back_tags[c])
             for t in range(PACK):
-                nc.tensor.transpose(back[:, t, :], pre[:, t, :], ident[:])
+                nc.tensor.transpose(back[:, t, :], values[:, t, :], ident[:])
+            backs.append(back)
+
+        def empty_bank(copy, c):
             result = keep.tile([P, PACK, P], F32, name=f"result{c}")
-            nc.scalar.activation(out=result[:], in_=back[:], func=SILU)
-            nc.sync.dma_start(out=out_view[:, :, cols], in_=result[:])
+            copy(out=result[:], in_=backs[c][:])
+            nc.sync.dma_start(out=out_view[:, :, c * P : (c + 1) * P], in_=result[:])
             results.append(result)
 
-        rounded = keep.tile([P, S, PACK], BF16, name="rounded", align_bytes=64)
-
-        def round_result(c):
+        def round_result(copy, c):
             dst, src = interleave_views(rounded[:, c * P : (c + 1) * P, :], results[c][:])
-            nc.vector.tensor_copy(out=dst, in_=src)
+            copy(out=dst, in_=src)
 
         def quantize_result(first, last):
             cols = slice(first * P, last * P)
@@ -189,14 +195,20 @@ def tile_picked_zdq_linsilu_po_kernel(
                 in_=rounded[:, cols, :].rearrange("p j t -> p (j t)"),
             )
 
+        def silu(out, in_):
+            nc.scalar.activation(out=out, in_=in_, func=SILU)
+
+        empty_bank(nc.vector.tensor_copy, 0)
+        empty_bank(silu, 1)
+        empty_bank(silu, 2)
+        empty_bank(silu, 3)
         for c in range(CHUNKS - 1):
-            round_result(c)
+            round_result(nc.vector.tensor_copy, c)
         quantize_result(0, 2)
-        nc.sync.dma_start(out=code_view[:, 0 : 2 * P], in_=out_codes[:, 0 : 2 * P].bitcast(I32))
-        round_result(CHUNKS - 1)
+        round_result(nc.scalar.copy, CHUNKS - 1)
         quantize_result(2, 3)
         quantize_result(3, 4)
-        nc.scalar.dma_start(out=code_view[:, 2 * P : S], in_=out_codes[:, 2 * P : S].bitcast(I32))
+        nc.scalar.dma_start(out=code_view, in_=out_codes[:].bitcast(I32))
         for q in range(QUADS):
             queue = nc.scalar if q == QUADS - 1 else nc.sync
             queue.dma_start(

@@ -1,7 +1,6 @@
 from contextlib import ExitStack
 
 import concourse.mybir as mybir
-from concourse.masks import make_identity
 
 K, T, S, N = 512, 1024, 512, 512
 FLOPS = 2 * K * S * N
@@ -15,18 +14,21 @@ U8 = mybir.dt.uint8
 FP8X4 = mybir.dt.float8_e4m3fn_x4
 MULT = mybir.AluOpType.mult
 ADD = mybir.AluOpType.add
+IS_EQUAL = mybir.AluOpType.is_equal
 SILU = mybir.ActivationFunctionType.Silu
 COPY = mybir.ActivationFunctionType.Copy
 
 P = 128
 PACK = 4
 QUADS = 4
+BLOCK = 32
 CHUNKS = S // P
 LIST_ROWS = 16
 LIST_COLS = P // LIST_ROWS
 HALF = N // 2
-EARLY = 1
-SHIFT_ROW = 64
+TABLE_ROWS = 16
+GAIN_ROW = P - 2 * TABLE_ROWS
+SHIFT_ROW = P - TABLE_ROWS
 SCALAR_SHARE = 192
 
 
@@ -43,7 +45,6 @@ def tile_picked_zdq_linsilu_po_kernel(
     nc = tc.nc
     with ExitStack() as ctx:
         keep = ctx.enter_context(tc.tile_pool(name="keep", bufs=1))
-        shared = ctx.enter_context(tc.tile_pool(name="shared", bufs=1))
         psum = ctx.enter_context(tc.psum_pool(name="psum", bufs=1))
 
         offsets = keep.tile([P, S // LIST_ROWS], U16, name="offsets")
@@ -52,25 +53,50 @@ def tile_picked_zdq_linsilu_po_kernel(
         byte_table = keep.tile([P, T], U8, name="byte_table")
         nc.vector.memset(byte_table[:].bitcast(I32), 0)
         row_table = keep.tile([P, T], F32, name="row_table")
-        nc.vector.memset(row_table[:].bitcast(I32), 0)
-        for q in range(QUADS):
-            queue = nc.sync if q < 2 else nc.scalar
+        nc.vector.memset(row_table[0:GAIN_ROW, :].bitcast(I32), 0)
+
+        def load_scale_rows(queue, q):
             queue.dma_start(
                 out=byte_table[32 * q : 32 * q + 4, :].bitcast(I32),
                 in_=x_scales[0, 4 * q : 4 * q + 4, :].bitcast(I32),
             )
-        nc.sync.dma_start(out=row_table[0:1, :], in_=gain[0:1, :])
-        nc.scalar.dma_start(out=row_table[SHIFT_ROW : SHIFT_ROW + 1, :], in_=shift[0:1, :])
+
+        load_scale_rows(nc.scalar, 1)
+        nc.scalar.dma_start(out=row_table[GAIN_ROW:SHIFT_ROW, :], in_=gain[0:TABLE_ROWS, :])
+        nc.sync.dma_start(out=row_table[SHIFT_ROW:P, :], in_=shift[0:TABLE_ROWS, :])
+        load_scale_rows(nc.sync, 0)
+        load_scale_rows(nc.scalar, 2)
+        load_scale_rows(nc.sync, 3)
 
         ident = keep.tile([P, P], F32, name="ident")
-        nc.vector.memset(ident[:], 0.0)
-        make_identity(nc, ident[:], nomemset=True)
-        warm = keep.tile([P, 8], F32, name="warm")
-        nc.vector.memset(warm[:], 0.0)
-        nc.scalar.activation(out=warm[:, 4:5], in_=warm[:, 0:1], func=SILU)
+        before_block = keep.tile([P, 1], F32, name="before_block")
+        for q in range(QUADS):
+            nc.gpsimd.memset(before_block[BLOCK * q : BLOCK * (q + 1), :], float(BLOCK * q))
+        ones = keep.tile([P, P], F32, name="ones")
+        nc.vector.memset(ones[:], 1.0)
+        block_count = keep.tile([P, BLOCK], F32, name="block_count", align_bytes=64)
+        row_count = keep.tile([P, BLOCK], F32, name="row_count", align_bytes=64)
+        col_count = keep.tile([P, P], F32, name="col_count")
+        nc.vector.tensor_tensor_scan(
+            out=block_count[:],
+            data0=ones[:, 0:BLOCK],
+            data1=ones[:, 0:BLOCK],
+            initial=before_block[:],
+            op0=MULT,
+            op1=ADD,
+        )
+        nc.vector.tensor_tensor_scan(
+            out=col_count[:], data0=ones[:], data1=ones[:], initial=0.0, op0=MULT, op1=ADD
+        )
+        nc.vector.transpose(out=row_count[:], in_=block_count[:])
+        nc.vector.tensor_scalar(
+            out=ident[:], in0=col_count[:], scalar1=row_count[:, 0:1], scalar2=None, op0=IS_EQUAL
+        )
+        warm = keep.tile([P, 1], F32, name="warm")
+        nc.scalar.activation(out=warm[:], in_=ones[:, 0:1], func=SILU)
 
         w_raw = keep.tile([P, PACK, N], F32, name="w_raw", tag="w_raw")
-        wsum_cols = shared.tile([P, PACK], F32, name="wsum_cols", offset=0, align_bytes=64)
+        wsum_cols = keep.tile([P, PACK], F32, name="wsum_cols")
         word_table = keep.tile([P, T], U32, name="word_table")
         nc.sync.dma_start(out=w_raw[:], in_=w1.rearrange("(p j) c -> p j c", j=PACK))
         nc.sync.dma_start(out=wsum_cols[:], in_=wsum.rearrange("(p t) o -> p (t o)", t=PACK))
@@ -78,11 +104,10 @@ def tile_picked_zdq_linsilu_po_kernel(
             out=word_table[:].bitcast(I32), in_=x_words[0].rearrange("p n t -> p (n t)").bitcast(I32)
         )
 
+        rows = keep.tile([P, S], F32, name="rows")
+        nc.vector.tensor_copy(out=rows[:], in_=row_table[:].indirect(offsets[:]))
         x_bytes = keep.tile([P, S], U8, name="x_bytes", align_bytes=64)
         nc.vector.tensor_copy(out=x_bytes[:], in_=byte_table[:].indirect(offsets[:]))
-
-        rows = shared.tile([P, S], F32, name="rows", offset=64, align_bytes=64)
-        nc.vector.tensor_copy(out=rows[:], in_=row_table[:].indirect(offsets[:]))
 
         turned = psum.tile([P, CHUNKS, P], F32, name="turned", tag="turned")
         for c in range(CHUNKS):
@@ -121,7 +146,7 @@ def tile_picked_zdq_linsilu_po_kernel(
                 stop=True,
             )
 
-        x_codes = shared.tile([P, S], U32, name="x_codes", offset=0, align_bytes=64)
+        x_codes = keep.tile([P, S], U32, name="x_codes", align_bytes=64)
         accs = [psum.tile([P, N], F32, name=f"acc{c}", tag=f"acc{c}") for c in range(CHUNKS)]
         for c in range(CHUNKS):
             cols = slice(c * P, (c + 1) * P)
@@ -142,7 +167,7 @@ def tile_picked_zdq_linsilu_po_kernel(
         late = keep.tile([P, CHUNKS * N + 2 * CHUNKS], F32, name="late", tag="w_raw")
         terms = late[:, 0 : CHUNKS * N].rearrange("p (c m) -> p c m", c=CHUNKS)
         factors = late[:, CHUNKS * N :].rearrange("p (c f) -> p c f", f=2)
-        nc.scalar.copy(out=factors, in_=turned[:, :, 0:P:SHIFT_ROW])
+        nc.scalar.copy(out=factors, in_=turned[:, :, GAIN_ROW:P:TABLE_ROWS])
         for c in range(CHUNKS):
             nc.scalar.activation(
                 out=terms[:, c, :],
@@ -155,10 +180,10 @@ def tile_picked_zdq_linsilu_po_kernel(
         code_view = out_1[0].rearrange("p n t -> p (n t)").bitcast(I32)
         out_codes = keep.tile([P, S], U32, name="out_codes", align_bytes=64)
         out_bytes = keep.tile([P, S], U8, name="out_bytes", align_bytes=64)
-        rounded = keep.tile([P, S, PACK], BF16, name="rounded", align_bytes=64)
         back_tags = ["back0", "back1", "turned", "acc0"]
-        backs, results = [], []
+        results = []
         for c in range(CHUNKS):
+            cols = slice(c * P, (c + 1) * P)
             pre = keep.tile([P, PACK, P], F32, name=f"pre{c}")
             nc.vector.scalar_tensor_tensor(
                 out=pre[:],
@@ -168,24 +193,19 @@ def tile_picked_zdq_linsilu_po_kernel(
                 op0=MULT,
                 op1=ADD,
             )
-            values = pre
-            if c < EARLY:
-                values = keep.tile([P, PACK, P], F32, name=f"values{c}")
-                nc.scalar.activation(out=values[:], in_=pre[:], func=SILU)
             back = psum.tile([P, PACK, P], F32, name=f"back{c}", tag=back_tags[c])
             for t in range(PACK):
-                nc.tensor.transpose(back[:, t, :], values[:, t, :], ident[:])
-            backs.append(back)
-
-        def empty_bank(copy, c):
+                nc.tensor.transpose(back[:, t, :], pre[:, t, :], ident[:])
             result = keep.tile([P, PACK, P], F32, name=f"result{c}")
-            copy(out=result[:], in_=backs[c][:])
-            nc.sync.dma_start(out=out_view[:, :, c * P : (c + 1) * P], in_=result[:])
+            nc.scalar.activation(out=result[:], in_=back[:], func=SILU)
+            nc.sync.dma_start(out=out_view[:, :, cols], in_=result[:])
             results.append(result)
 
-        def round_result(copy, c):
+        rounded = keep.tile([P, S, PACK], BF16, name="rounded", align_bytes=64)
+
+        def round_result(c):
             dst, src = interleave_views(rounded[:, c * P : (c + 1) * P, :], results[c][:])
-            copy(out=dst, in_=src)
+            nc.vector.tensor_copy(out=dst, in_=src)
 
         def quantize_result(first, last):
             cols = slice(first * P, last * P)
@@ -195,20 +215,14 @@ def tile_picked_zdq_linsilu_po_kernel(
                 in_=rounded[:, cols, :].rearrange("p j t -> p (j t)"),
             )
 
-        def silu(out, in_):
-            nc.scalar.activation(out=out, in_=in_, func=SILU)
-
-        empty_bank(nc.vector.tensor_copy, 0)
-        empty_bank(silu, 1)
-        empty_bank(silu, 2)
-        empty_bank(silu, 3)
         for c in range(CHUNKS - 1):
-            round_result(nc.vector.tensor_copy, c)
+            round_result(c)
         quantize_result(0, 2)
-        round_result(nc.scalar.copy, CHUNKS - 1)
+        nc.sync.dma_start(out=code_view[:, 0 : 2 * P], in_=out_codes[:, 0 : 2 * P].bitcast(I32))
+        round_result(CHUNKS - 1)
         quantize_result(2, 3)
         quantize_result(3, 4)
-        nc.scalar.dma_start(out=code_view, in_=out_codes[:].bitcast(I32))
+        nc.scalar.dma_start(out=code_view[:, 2 * P : S], in_=out_codes[:, 2 * P : S].bitcast(I32))
         for q in range(QUADS):
             queue = nc.scalar if q == QUADS - 1 else nc.sync
             queue.dma_start(

@@ -26,9 +26,8 @@ CHUNKS = S // P
 LIST_ROWS = 16
 LIST_COLS = P // LIST_ROWS
 HALF = N // 2
-TABLE_ROWS = 16
-GAIN_ROW = P - 2 * TABLE_ROWS
-SHIFT_ROW = P - TABLE_ROWS
+GAIN_ROW = P - 2
+SHIFT_ROW = P - 1
 SCALAR_SHARE = 192
 
 
@@ -53,7 +52,6 @@ def tile_picked_zdq_linsilu_po_kernel(
         byte_table = keep.tile([P, T], U8, name="byte_table")
         nc.vector.memset(byte_table[:].bitcast(I32), 0)
         row_table = keep.tile([P, T], F32, name="row_table")
-        nc.vector.memset(row_table[0:GAIN_ROW, :].bitcast(I32), 0)
 
         def load_scale_rows(queue, q):
             queue.dma_start(
@@ -61,12 +59,10 @@ def tile_picked_zdq_linsilu_po_kernel(
                 in_=x_scales[0, 4 * q : 4 * q + 4, :].bitcast(I32),
             )
 
-        load_scale_rows(nc.scalar, 1)
-        nc.scalar.dma_start(out=row_table[GAIN_ROW:SHIFT_ROW, :], in_=gain[0:TABLE_ROWS, :])
-        nc.sync.dma_start(out=row_table[SHIFT_ROW:P, :], in_=shift[0:TABLE_ROWS, :])
-        load_scale_rows(nc.sync, 0)
-        load_scale_rows(nc.scalar, 2)
-        load_scale_rows(nc.sync, 3)
+        nc.scalar.dma_start(out=row_table[GAIN_ROW:SHIFT_ROW, :], in_=gain[0:1, :])
+        nc.scalar.dma_start(out=row_table[SHIFT_ROW:P, :], in_=shift[0:1, :])
+        for q in range(QUADS):
+            load_scale_rows(nc.sync if q % 2 == 0 else nc.scalar, q)
 
         ident = keep.tile([P, P], F32, name="ident")
         before_block = keep.tile([P, 1], F32, name="before_block")
@@ -92,6 +88,8 @@ def tile_picked_zdq_linsilu_po_kernel(
         nc.vector.tensor_scalar(
             out=ident[:], in0=col_count[:], scalar1=row_count[:, 0:1], scalar2=None, op0=IS_EQUAL
         )
+        for q in range(QUADS):
+            nc.vector.memset(row_table[0:GAIN_ROW, q * T // QUADS : (q + 1) * T // QUADS].bitcast(I32), 0)
         warm = keep.tile([P, 1], F32, name="warm")
         nc.scalar.activation(out=warm[:], in_=ones[:, 0:1], func=SILU)
 
@@ -167,7 +165,7 @@ def tile_picked_zdq_linsilu_po_kernel(
         late = keep.tile([P, CHUNKS * N + 2 * CHUNKS], F32, name="late", tag="w_raw")
         terms = late[:, 0 : CHUNKS * N].rearrange("p (c m) -> p c m", c=CHUNKS)
         factors = late[:, CHUNKS * N :].rearrange("p (c f) -> p c f", f=2)
-        nc.scalar.copy(out=factors, in_=turned[:, :, GAIN_ROW:P:TABLE_ROWS])
+        nc.scalar.copy(out=factors, in_=turned[:, :, GAIN_ROW:P])
         for c in range(CHUNKS):
             nc.scalar.activation(
                 out=terms[:, c, :],

@@ -103,7 +103,7 @@ def tile_picked_zdq_linsilu_po_kernel(
         )
 
         rows = keep.tile([P, S], F32, name="rows")
-        nc.vector.tensor_copy(out=rows[:], in_=row_table[:].indirect(offsets[:]))
+        nc.scalar.activation(out=rows[:], in_=row_table[:].indirect(offsets[:]), func=COPY)
         x_bytes = keep.tile([P, S], U8, name="x_bytes", align_bytes=64)
         nc.vector.tensor_copy(out=x_bytes[:], in_=byte_table[:].indirect(offsets[:]))
 
@@ -132,17 +132,16 @@ def tile_picked_zdq_linsilu_po_kernel(
                 in_=w_rounded[:, cols, :].rearrange("p c j -> p (c j)"),
             )
 
-        unread = psum.tile([P, N], F32, name="unread", tag="back0")
-        for h in range(2):
-            nc.tensor.matmul_mx(
-                out=unread[:, h * HALF : (h + 1) * HALF],
-                lhsT=w_codes[:, 0:P].bitcast(FP8X4),
-                lhsT_scale=w_bytes[:, 0:P],
-                rhs=w_codes[:, 0:HALF].bitcast(FP8X4),
-                rhs_scale=w_bytes[:, 0:HALF],
-                start=True,
-                stop=True,
-            )
+        unread = psum.tile([P, HALF], F32, name="unread", tag="back0")
+        nc.tensor.matmul_mx(
+            out=unread[:],
+            lhsT=w_codes[:, 0:P].bitcast(FP8X4),
+            lhsT_scale=w_bytes[:, 0:P],
+            rhs=w_codes[:, 0:HALF].bitcast(FP8X4),
+            rhs_scale=w_bytes[:, 0:HALF],
+            start=True,
+            stop=True,
+        )
 
         x_codes = keep.tile([P, S], U32, name="x_codes", align_bytes=64)
         accs = [psum.tile([P, N], F32, name=f"acc{c}", tag=f"acc{c}") for c in range(CHUNKS)]

@@ -178,7 +178,8 @@ def tile_picked_zdq_linsilu_po_kernel(
         out_codes = keep.tile([P, S], U32, name="out_codes", align_bytes=64)
         out_bytes = keep.tile([P, S], U8, name="out_bytes", align_bytes=64)
         back_tags = ["back0", "back1", "turned", "acc0"]
-        results = []
+        result = keep.tile([P, PACK, S], F32, name="result")
+        stores = {0: slice(0, P), 1: slice(P, 2 * P), 3: slice(2 * P, S)}
         for c in range(CHUNKS):
             cols = slice(c * P, (c + 1) * P)
             pre = keep.tile([P, PACK, P], F32, name=f"pre{c}")
@@ -193,15 +194,14 @@ def tile_picked_zdq_linsilu_po_kernel(
             back = psum.tile([P, PACK, P], F32, name=f"back{c}", tag=back_tags[c])
             for t in range(PACK):
                 nc.tensor.transpose(back[:, t, :], pre[:, t, :], ident[:])
-            result = keep.tile([P, PACK, P], F32, name=f"result{c}")
-            nc.scalar.activation(out=result[:], in_=back[:], func=SILU)
-            nc.sync.dma_start(out=out_view[:, :, cols], in_=result[:])
-            results.append(result)
+            nc.scalar.activation(out=result[:, :, cols], in_=back[:], func=SILU)
+            if c in stores:
+                nc.sync.dma_start(out=out_view[:, :, stores[c]], in_=result[:, :, stores[c]])
 
         rounded = keep.tile([P, S, PACK], BF16, name="rounded", align_bytes=64)
 
         def round_result(c):
-            dst, src = interleave_views(rounded[:, c * P : (c + 1) * P, :], results[c][:])
+            dst, src = interleave_views(rounded[:, c * P : (c + 1) * P, :], result[:, :, c * P : (c + 1) * P])
             nc.vector.tensor_copy(out=dst, in_=src)
 
         def quantize_result(first, last):

@@ -110,7 +110,7 @@ def tile_picked_zdq_linsilu_po_kernel(
         turned = psum.tile([P, CHUNKS, P], F32, name="turned", tag="turned")
         for c in range(CHUNKS):
             nc.tensor.transpose(turned[:, c, :], rows[:, c * P : (c + 1) * P], ident[:])
-        wsum_rows = psum.tile([P, PACK, P], F32, name="wsum_rows")
+        wsum_rows = psum.tile([P, PACK, P], F32, name="wsum_rows", tag="wsum_rows")
         for t in range(PACK):
             nc.tensor.transpose(wsum_rows[:, t, :], wsum_cols[:, t : t + 1].to_broadcast([P, P]), ident[:])
 
@@ -177,7 +177,7 @@ def tile_picked_zdq_linsilu_po_kernel(
         code_view = out_1[0].rearrange("p n t -> p (n t)").bitcast(I32)
         out_codes = keep.tile([P, S], U32, name="out_codes", align_bytes=64)
         out_bytes = keep.tile([P, S], U8, name="out_bytes", align_bytes=64)
-        back_tags = ["back0", "back1", "turned", "acc0"]
+        back_tags = [["back0", "back1"], ["turned"], ["wsum_rows"], ["acc0"]]
         result = keep.tile([P, PACK, S], F32, name="result")
         stores = {0: slice(0, P), 1: slice(P, 2 * P), 3: slice(2 * P, S)}
         for c in range(CHUNKS):
@@ -191,10 +191,12 @@ def tile_picked_zdq_linsilu_po_kernel(
                 op0=MULT,
                 op1=ADD,
             )
-            back = psum.tile([P, PACK, P], F32, name=f"back{c}", tag=back_tags[c])
-            for t in range(PACK):
-                nc.tensor.transpose(back[:, t, :], pre[:, t, :], ident[:])
-            nc.scalar.activation(out=result[:, :, cols], in_=back[:], func=SILU)
+            slots = PACK // len(back_tags[c])
+            for b, tag in enumerate(back_tags[c]):
+                back = psum.tile([P, slots, P], F32, name=f"back{c}_{b}", tag=tag)
+                for t in range(slots):
+                    nc.tensor.transpose(back[:, t, :], pre[:, b * slots + t, :], ident[:])
+                nc.scalar.activation(out=result[:, b * slots : (b + 1) * slots, cols], in_=back[:], func=SILU)
             if c in stores:
                 nc.sync.dma_start(out=out_view[:, :, stores[c]], in_=result[:, :, stores[c]])
 

@@ -177,7 +177,7 @@ def tile_picked_zdq_linsilu_po_kernel(
         code_view = out_1[0].rearrange("p n t -> p (n t)").bitcast(I32)
         out_codes = keep.tile([P, S], U32, name="out_codes", align_bytes=64)
         out_bytes = keep.tile([P, S], U8, name="out_bytes", align_bytes=64)
-        back_tags = [["back0", "back1"], ["turned"], ["wsum_rows"], ["acc0"]]
+        back_tags = [["back0", "back1"], ["turned", "wsum_rows"], ["acc0", "acc1"], ["acc2"]]
         result = keep.tile([P, PACK, S], F32, name="result")
         stores = {0: slice(0, P), 1: slice(P, 2 * P), 3: slice(2 * P, S)}
         for c in range(CHUNKS):
@@ -196,32 +196,40 @@ def tile_picked_zdq_linsilu_po_kernel(
                 back = psum.tile([P, slots, P], F32, name=f"back{c}_{b}", tag=tag)
                 for t in range(slots):
                     nc.tensor.transpose(back[:, t, :], pre[:, b * slots + t, :], ident[:])
-                nc.scalar.activation(out=result[:, b * slots : (b + 1) * slots, cols], in_=back[:], func=SILU)
+                width = P // 2 if c == CHUNKS - 1 else P
+                for j in range(0, P, width):
+                    nc.scalar.activation(
+                        out=result[:, b * slots : (b + 1) * slots, c * P + j : c * P + j + width],
+                        in_=back[:, :, j : j + width],
+                        func=SILU,
+                    )
             if c in stores:
                 nc.sync.dma_start(out=out_view[:, :, stores[c]], in_=result[:, :, stores[c]])
 
         rounded = keep.tile([P, S, PACK], BF16, name="rounded", align_bytes=64)
 
-        def round_result(c):
-            dst, src = interleave_views(rounded[:, c * P : (c + 1) * P, :], result[:, :, c * P : (c + 1) * P])
+        def round_result(cols):
+            dst, src = interleave_views(rounded[:, cols, :], result[:, :, cols])
             nc.vector.tensor_copy(out=dst, in_=src)
 
-        def quantize_result(first, last):
-            cols = slice(first * P, last * P)
+        def quantize_result(cols):
             nc.vector.quantize_mx(
                 out=out_codes[:, cols].bitcast(FP8X4),
                 scales=out_bytes[:, cols],
                 in_=rounded[:, cols, :].rearrange("p j t -> p (j t)"),
             )
 
-        for c in range(CHUNKS - 1):
-            round_result(c)
-        quantize_result(0, 2)
-        nc.sync.dma_start(out=code_view[:, 0 : 2 * P], in_=out_codes[:, 0 : 2 * P].bitcast(I32))
-        round_result(CHUNKS - 1)
-        quantize_result(2, 3)
-        quantize_result(3, 4)
-        nc.scalar.dma_start(out=code_view[:, 2 * P : S], in_=out_codes[:, 2 * P : S].bitcast(I32))
+        early = S // 2
+        for first in range(0, S, early):
+            for start in range(first, first + early, P):
+                middle = start + P // 2
+                round_result(slice(start, middle))
+                round_result(slice(middle, start + P))
+                quantize_result(slice(max(middle - P, first), middle))
+            quantize_result(slice(first + early - P // 2, first + early))
+            if first == 0:
+                nc.sync.dma_start(out=code_view[:, 0:early], in_=out_codes[:, 0:early].bitcast(I32))
+        nc.scalar.dma_start(out=code_view[:, early:S], in_=out_codes[:, early:S].bitcast(I32))
         for q in range(QUADS):
             queue = nc.scalar if q == QUADS - 1 else nc.sync
             queue.dma_start(

@@ -60,14 +60,14 @@ def tile_picked_zdq_linsilu_po_kernel(
             )
 
         nc.scalar.dma_start(out=row_table[GAIN_ROW:SHIFT_ROW, :], in_=gain[0:1, :])
-        nc.scalar.dma_start(out=row_table[SHIFT_ROW:P, :], in_=shift[0:1, :])
+        nc.sync.dma_start(out=row_table[SHIFT_ROW:P, :], in_=shift[0:1, :])
         for q in range(QUADS):
             load_scale_rows(nc.sync if q % 2 == 0 else nc.scalar, q)
 
         ident = keep.tile([P, P], F32, name="ident")
         before_block = keep.tile([P, 1], F32, name="before_block")
         for q in range(QUADS):
-            nc.gpsimd.memset(before_block[BLOCK * q : BLOCK * (q + 1), :], float(BLOCK * q))
+            nc.vector.memset(before_block[BLOCK * q : BLOCK * (q + 1), :], float(BLOCK * q))
         ones = keep.tile([P, P], F32, name="ones")
         nc.vector.memset(ones[:], 1.0)
         block_count = keep.tile([P, BLOCK], F32, name="block_count", align_bytes=64)

@@ -177,34 +177,38 @@ def tile_picked_zdq_linsilu_po_kernel(
         code_view = out_1[0].rearrange("p n t -> p (n t)").bitcast(I32)
         out_codes = keep.tile([P, S], U32, name="out_codes", align_bytes=64)
         out_bytes = keep.tile([P, S], U8, name="out_bytes", align_bytes=64)
-        back_tags = [["back0", "back1"], ["turned", "wsum_rows"], ["acc0", "acc1"], ["acc2"]]
         result = keep.tile([P, PACK, S], F32, name="result")
-        stores = {0: slice(0, P), 1: slice(P, 2 * P), 3: slice(2 * P, S)}
+        pre = []
         for c in range(CHUNKS):
-            cols = slice(c * P, (c + 1) * P)
-            pre = keep.tile([P, PACK, P], F32, name=f"pre{c}")
+            pre.append(keep.tile([P, PACK, P], F32, name=f"pre{c}"))
             nc.vector.scalar_tensor_tensor(
-                out=pre[:],
+                out=pre[c][:],
                 in0=accs[c][:].rearrange("p (m t) -> p t m", t=PACK),
                 scalar=factors[:, c, 0:1],
                 in1=terms[:, c, :].rearrange("p (t m) -> p t m", t=PACK),
                 op0=MULT,
                 op1=ADD,
             )
-            slots = PACK // len(back_tags[c])
-            for b, tag in enumerate(back_tags[c]):
-                back = psum.tile([P, slots, P], F32, name=f"back{c}_{b}", tag=tag)
-                for t in range(slots):
-                    nc.tensor.transpose(back[:, t, :], pre[:, b * slots + t, :], ident[:])
-                width = P // 2 if c == CHUNKS - 1 else P
-                for j in range(0, P, width):
-                    nc.scalar.activation(
-                        out=result[:, b * slots : (b + 1) * slots, c * P + j : c * P + j + width],
-                        in_=back[:, :, j : j + width],
-                        func=SILU,
-                    )
-            if c in stores:
-                nc.sync.dma_start(out=out_view[:, :, stores[c]], in_=result[:, :, stores[c]])
+
+        def turn_back(c, first, slots, tag, width=P):
+            back = psum.tile([P, slots, P], F32, name=f"back{c}_{first}", tag=tag)
+            for t in range(slots):
+                nc.tensor.transpose(back[:, t, :], pre[c][:, first + t, :], ident[:])
+            for j in range(0, P, width):
+                nc.scalar.activation(
+                    out=result[:, first : first + slots, c * P + j : c * P + j + width],
+                    in_=back[:, :, j : j + width],
+                    func=SILU,
+                )
+
+        for first, tags in ((0, ("back0", "back1")), (2, ("acc1", "turned"))):
+            for c in range(2):
+                turn_back(c, first, 2, tags[c])
+            nc.sync.dma_start(out=out_view[:, first : first + 2, 0 : 2 * P], in_=result[:, first : first + 2, 0 : 2 * P])
+        turn_back(2, 0, 2, "wsum_rows")
+        turn_back(2, 2, 2, "acc0")
+        turn_back(3, 0, PACK, "acc2", P // 2)
+        nc.sync.dma_start(out=out_view[:, :, 2 * P : S], in_=result[:, :, 2 * P : S])
 
         rounded = keep.tile([P, S, PACK], BF16, name="rounded", align_bytes=64)
 

@@ -181,14 +181,15 @@ def tile_picked_zdq_linsilu_po_kernel(
         pre = []
         for c in range(CHUNKS):
             pre.append(keep.tile([P, PACK, P], F32, name=f"pre{c}"))
-            nc.vector.scalar_tensor_tensor(
-                out=pre[c][:],
-                in0=accs[c][:].rearrange("p (m t) -> p t m", t=PACK),
-                scalar=factors[:, c, 0:1],
-                in1=terms[:, c, :].rearrange("p (t m) -> p t m", t=PACK),
-                op0=MULT,
-                op1=ADD,
-            )
+            for slots in (slice(0, 2), slice(2, PACK)) if c == 1 else (slice(0, PACK),):
+                nc.vector.scalar_tensor_tensor(
+                    out=pre[c][:, slots, :],
+                    in0=accs[c][:].rearrange("p (m t) -> p t m", t=PACK)[:, slots, :],
+                    scalar=factors[:, c, 0:1],
+                    in1=terms[:, c, :].rearrange("p (t m) -> p t m", t=PACK)[:, slots, :],
+                    op0=MULT,
+                    op1=ADD,
+                )
 
         def turn_back(c, first, slots, tag, width=P):
             back = psum.tile([P, slots, P], F32, name=f"back{c}_{first}", tag=tag)
@@ -207,14 +208,15 @@ def tile_picked_zdq_linsilu_po_kernel(
             nc.sync.dma_start(out=out_view[:, first : first + 2, 0 : 2 * P], in_=result[:, first : first + 2, 0 : 2 * P])
         turn_back(2, 0, 2, "wsum_rows")
         turn_back(2, 2, 2, "acc0")
-        turn_back(3, 0, PACK, "acc2", P // 2)
-        nc.sync.dma_start(out=out_view[:, :, 2 * P : S], in_=result[:, :, 2 * P : S])
+        for first, tag in ((0, "acc2"), (2, "back0")):
+            turn_back(3, first, 2, tag)
+            nc.sync.dma_start(out=out_view[:, first : first + 2, 2 * P : S], in_=result[:, first : first + 2, 2 * P : S])
 
         rounded = keep.tile([P, S, PACK], BF16, name="rounded", align_bytes=64)
 
-        def round_result(cols):
+        def round_result(copy, cols):
             dst, src = interleave_views(rounded[:, cols, :], result[:, :, cols])
-            nc.vector.tensor_copy(out=dst, in_=src)
+            copy(out=dst, in_=src)
 
         def quantize_result(cols):
             nc.vector.quantize_mx(
@@ -223,17 +225,14 @@ def tile_picked_zdq_linsilu_po_kernel(
                 in_=rounded[:, cols, :].rearrange("p j t -> p (j t)"),
             )
 
-        early = S // 2
-        for first in range(0, S, early):
-            for start in range(first, first + early, P):
-                middle = start + P // 2
-                round_result(slice(start, middle))
-                round_result(slice(middle, start + P))
-                quantize_result(slice(max(middle - P, first), middle))
-            quantize_result(slice(first + early - P // 2, first + early))
-            if first == 0:
-                nc.sync.dma_start(out=code_view[:, 0:early], in_=out_codes[:, 0:early].bitcast(I32))
-        nc.scalar.dma_start(out=code_view[:, early:S], in_=out_codes[:, early:S].bitcast(I32))
+        for start in range(0, S, P):
+            middle = start + P // 2
+            copy = nc.scalar.copy if start == S - P else nc.vector.tensor_copy
+            round_result(copy, slice(start, middle))
+            round_result(copy, slice(middle, start + P))
+            quantize_result(slice(max(middle - P, 0), middle))
+        quantize_result(slice(S - P // 2, S))
+        nc.scalar.dma_start(out=code_view, in_=out_codes[:].bitcast(I32))
         for q in range(QUADS):
             queue = nc.scalar if q == QUADS - 1 else nc.sync
             queue.dma_start(

@@ -211,12 +211,15 @@ def tile_picked_zdq_linsilu_po_kernel(
         for first, tag in ((0, "acc2"), (2, "back0")):
             turn_back(3, first, 2, tag)
             nc.sync.dma_start(out=out_view[:, first : first + 2, 2 * P : S], in_=result[:, first : first + 2, 2 * P : S])
+        last_back = psum.tile([P, PACK, P], F32, name="last_back", tag="back1")
+        for t in range(PACK):
+            nc.tensor.transpose(last_back[:, t, :], pre[3][:, t, :], ident[:])
 
         rounded = keep.tile([P, S, PACK], BF16, name="rounded", align_bytes=64)
 
-        def round_result(copy, cols):
+        def round_result(cols):
             dst, src = interleave_views(rounded[:, cols, :], result[:, :, cols])
-            copy(out=dst, in_=src)
+            nc.vector.tensor_copy(out=dst, in_=src)
 
         def quantize_result(cols):
             nc.vector.quantize_mx(
@@ -225,13 +228,13 @@ def tile_picked_zdq_linsilu_po_kernel(
                 in_=rounded[:, cols, :].rearrange("p j t -> p (j t)"),
             )
 
-        for start in range(0, S, P):
-            middle = start + P // 2
-            copy = nc.scalar.copy if start == S - P else nc.vector.tensor_copy
-            round_result(copy, slice(start, middle))
-            round_result(copy, slice(middle, start + P))
-            quantize_result(slice(max(middle - P, 0), middle))
-        quantize_result(slice(S - P // 2, S))
+        nc.scalar.activation(out=rounded[:, S - P : S, :], in_=last_back[:].rearrange("p t j -> p j t"), func=SILU)
+        groups = (slice(0, 2 * P), slice(2 * P, S - P))
+        for cols in groups:
+            round_result(cols)
+        for cols in groups:
+            quantize_result(cols)
+        quantize_result(slice(S - P, S))
         nc.scalar.dma_start(out=code_view, in_=out_codes[:].bitcast(I32))
         for q in range(QUADS):
             queue = nc.scalar if q == QUADS - 1 else nc.sync

from contextlib import ExitStack

import concourse.mybir as mybir

K, T, S, N = 512, 1024, 512, 512
FLOPS = 2 * K * S * N

F32 = mybir.dt.float32
BF16 = mybir.dt.bfloat16
I32 = mybir.dt.int32
U32 = mybir.dt.uint32
U16 = mybir.dt.uint16
U8 = mybir.dt.uint8
FP8X4 = mybir.dt.float8_e4m3fn_x4
MULT = mybir.AluOpType.mult
ADD = mybir.AluOpType.add
IS_EQUAL = mybir.AluOpType.is_equal
SILU = mybir.ActivationFunctionType.Silu
COPY = mybir.ActivationFunctionType.Copy

P = 128
PACK = 4
QUADS = 4
BLOCK = 32
CHUNKS = S // P
LIST_ROWS = 16
LIST_COLS = P // LIST_ROWS
HALF = N // 2
GAIN_ROW = P - 2
SHIFT_ROW = P - 1
SCALAR_SHARE = 192


def interleave_views(dst, src):
    return (
        dst.rearrange("p (c i) t -> p c t i", i=4),
        src.rearrange("p t (c i) -> p c t i", i=4),
    )


def tile_picked_zdq_linsilu_po_kernel(
    tc, x_words, x_scales, w1, gain, shift, wsum, offs, out_0, out_1, out_2
):
    nc = tc.nc
    with ExitStack() as ctx:
        keep = ctx.enter_context(tc.tile_pool(name="keep", bufs=1))
        psum = ctx.enter_context(tc.psum_pool(name="psum", bufs=1))

        offsets = keep.tile([P, S // LIST_ROWS], U16, name="offsets")
        nc.sync.dma_start(offsets[:], offs)

        byte_table = keep.tile([P, T], U8, name="byte_table")
        nc.vector.memset(byte_table[:].bitcast(I32), 0)
        row_table = keep.tile([P, T], F32, name="row_table")

        def load_scale_rows(queue, q):
            queue.dma_start(
                out=byte_table[32 * q : 32 * q + 4, :].bitcast(I32),
                in_=x_scales[0, 4 * q : 4 * q + 4, :].bitcast(I32),
            )

        nc.scalar.dma_start(out=row_table[GAIN_ROW:SHIFT_ROW, :], in_=gain[0:1, :])
        nc.sync.dma_start(out=row_table[SHIFT_ROW:P, :], in_=shift[0:1, :])
        for q in range(QUADS):
            load_scale_rows(nc.sync if q % 2 == 0 else nc.scalar, q)

        ident = keep.tile([P, P], F32, name="ident")
        before_block = keep.tile([P, 1], F32, name="before_block")
        for q in range(QUADS):
            nc.vector.memset(before_block[BLOCK * q : BLOCK * (q + 1), :], float(BLOCK * q))
        ones = keep.tile([P, P], F32, name="ones")
        nc.vector.memset(ones[:], 1.0)
        block_count = keep.tile([P, BLOCK], F32, name="block_count", align_bytes=64)
        row_count = keep.tile([P, BLOCK], F32, name="row_count", align_bytes=64)
        col_count = keep.tile([P, P], F32, name="col_count")
        nc.vector.tensor_tensor_scan(
            out=block_count[:],
            data0=ones[:, 0:BLOCK],
            data1=ones[:, 0:BLOCK],
            initial=before_block[:],
            op0=MULT,
            op1=ADD,
        )
        nc.vector.tensor_tensor_scan(
            out=col_count[:], data0=ones[:], data1=ones[:], initial=0.0, op0=MULT, op1=ADD
        )
        nc.vector.transpose(out=row_count[:], in_=block_count[:])
        nc.vector.tensor_scalar(
            out=ident[:], in0=col_count[:], scalar1=row_count[:, 0:1], scalar2=None, op0=IS_EQUAL
        )
        for q in range(QUADS):
            nc.vector.memset(row_table[0:GAIN_ROW, q * T // QUADS : (q + 1) * T // QUADS].bitcast(I32), 0)
        warm = keep.tile([P, 1], F32, name="warm")
        nc.scalar.activation(out=warm[:], in_=ones[:, 0:1], func=SILU)

        w_raw = keep.tile([P, PACK, N], F32, name="w_raw", tag="w_raw")
        wsum_cols = keep.tile([P, PACK], F32, name="wsum_cols")
        word_table = keep.tile([P, T], U32, name="word_table")
        nc.sync.dma_start(out=w_raw[:], in_=w1.rearrange("(p j) c -> p j c", j=PACK))
        nc.sync.dma_start(out=wsum_cols[:], in_=wsum.rearrange("(p t) o -> p (t o)", t=PACK))
        nc.sync.dma_start(
            out=word_table[:].bitcast(I32), in_=x_words[0].rearrange("p n t -> p (n t)").bitcast(I32)
        )

        rows = keep.tile([P, S], F32, name="rows")
        nc.scalar.activation(out=rows[:], in_=row_table[:].indirect(offsets[:]), func=COPY)
        x_bytes = keep.tile([P, S], U8, name="x_bytes", align_bytes=64)
        nc.vector.tensor_copy(out=x_bytes[:], in_=byte_table[:].indirect(offsets[:]))

        turned = psum.tile([P, CHUNKS, P], F32, name="turned", tag="turned")
        for c in range(CHUNKS):
            nc.tensor.transpose(turned[:, c, :], rows[:, c * P : (c + 1) * P], ident[:])
        wsum_rows = psum.tile([P, PACK, P], F32, name="wsum_rows", tag="wsum_rows")
        for t in range(PACK):
            nc.tensor.transpose(wsum_rows[:, t, :], wsum_cols[:, t : t + 1].to_broadcast([P, P]), ident[:])

        w_rounded = keep.tile([P, N, PACK], BF16, name="w_rounded", align_bytes=64)
        w_codes = keep.tile([P, N], U32, name="w_codes", align_bytes=64)
        w_bytes = keep.tile([P, N], U8, name="w_bytes", align_bytes=64)
        for copy, cols in (
            (nc.vector.tensor_copy, slice(0, HALF)),
            (nc.vector.tensor_copy, slice(HALF, N - SCALAR_SHARE)),
            (nc.scalar.copy, slice(N - SCALAR_SHARE, N)),
        ):
            dst, src = interleave_views(w_rounded[:, cols, :], w_raw[:, :, cols])
            copy(out=dst, in_=src)
        for h in range(2):
            cols = slice(h * HALF, (h + 1) * HALF)
            nc.vector.quantize_mx(
                out=w_codes[:, cols].bitcast(FP8X4),
                scales=w_bytes[:, cols],
                in_=w_rounded[:, cols, :].rearrange("p c j -> p (c j)"),
            )

        unread = psum.tile([P, HALF], F32, name="unread", tag="back0")
        nc.tensor.matmul_mx(
            out=unread[:],
            lhsT=w_codes[:, 0:P].bitcast(FP8X4),
            lhsT_scale=w_bytes[:, 0:P],
            rhs=w_codes[:, 0:HALF].bitcast(FP8X4),
            rhs_scale=w_bytes[:, 0:HALF],
            start=True,
            stop=True,
        )

        x_codes = keep.tile([P, S], U32, name="x_codes", align_bytes=64)
        accs = [psum.tile([P, N], F32, name=f"acc{c}", tag=f"acc{c}") for c in range(CHUNKS)]
        for c in range(CHUNKS):
            cols = slice(c * P, (c + 1) * P)
            nc.vector.tensor_copy(
                out=x_codes[:, cols],
                in_=word_table[:].indirect(offsets[:, c * LIST_COLS : (c + 1) * LIST_COLS]),
            )
            nc.tensor.matmul_mx(
                out=accs[c][:],
                lhsT=x_codes[:, cols].bitcast(FP8X4),
                lhsT_scale=x_bytes[:, cols],
                rhs=w_codes[:].bitcast(FP8X4),
                rhs_scale=w_bytes[:],
                start=True,
                stop=True,
            )

        late = keep.tile([P, CHUNKS * N + 2 * CHUNKS], F32, name="late", tag="w_raw")
        terms = late[:, 0 : CHUNKS * N].rearrange("p (c m) -> p c m", c=CHUNKS)
        factors = late[:, CHUNKS * N :].rearrange("p (c f) -> p c f", f=2)
        nc.scalar.copy(out=factors, in_=turned[:, :, GAIN_ROW:P])
        for c in range(CHUNKS):
            nc.scalar.activation(
                out=terms[:, c, :],
                in_=wsum_rows[:].rearrange("p t m -> p (t m)"),
                func=COPY,
                scale=factors[:, c, 1:2],
            )

        out_view = out_0.rearrange("(p t) j -> p t j", t=PACK)
        code_view = out_1[0].rearrange("p n t -> p (n t)").bitcast(I32)
        out_codes = keep.tile([P, S], U32, name="out_codes", align_bytes=64)
        out_bytes = keep.tile([P, S], U8, name="out_bytes", align_bytes=64)
        result = keep.tile([P, PACK, S], F32, name="result")
        pre = []
        for c in range(CHUNKS):
            pre.append(keep.tile([P, PACK, P], F32, name=f"pre{c}"))
            for slots in (slice(0, 2), slice(2, PACK)) if c == 1 else (slice(0, PACK),):
                nc.vector.scalar_tensor_tensor(
                    out=pre[c][:, slots, :],
                    in0=accs[c][:].rearrange("p (m t) -> p t m", t=PACK)[:, slots, :],
                    scalar=factors[:, c, 0:1],
                    in1=terms[:, c, :].rearrange("p (t m) -> p t m", t=PACK)[:, slots, :],
                    op0=MULT,
                    op1=ADD,
                )

        def turn_back(c, first, slots, tag, width=P):
            back = psum.tile([P, slots, P], F32, name=f"back{c}_{first}", tag=tag)
            for t in range(slots):
                nc.tensor.transpose(back[:, t, :], pre[c][:, first + t, :], ident[:])
            for j in range(0, P, width):
                nc.scalar.activation(
                    out=result[:, first : first + slots, c * P + j : c * P + j + width],
                    in_=back[:, :, j : j + width],
                    func=SILU,
                )

        for first, tags in ((0, ("back0", "back1")), (2, ("acc1", "turned"))):
            for c in range(2):
                turn_back(c, first, 2, tags[c])
            nc.sync.dma_start(out=out_view[:, first : first + 2, 0 : 2 * P], in_=result[:, first : first + 2, 0 : 2 * P])
        turn_back(2, 0, 2, "wsum_rows")
        turn_back(2, 2, 2, "acc0")
        for first, tag in ((0, "acc2"), (2, "back0")):
            turn_back(3, first, 2, tag)
            nc.sync.dma_start(out=out_view[:, first : first + 2, 2 * P : S], in_=result[:, first : first + 2, 2 * P : S])
        last_back = psum.tile([P, PACK, P], F32, name="last_back", tag="back1")
        for t in range(PACK):
            nc.tensor.transpose(last_back[:, t, :], pre[3][:, t, :], ident[:])

        rounded = keep.tile([P, S, PACK], BF16, name="rounded", align_bytes=64)

        def round_result(cols):
            dst, src = interleave_views(rounded[:, cols, :], result[:, :, cols])
            nc.vector.tensor_copy(out=dst, in_=src)

        def quantize_result(cols):
            nc.vector.quantize_mx(
                out=out_codes[:, cols].bitcast(FP8X4),
                scales=out_bytes[:, cols],
                in_=rounded[:, cols, :].rearrange("p j t -> p (j t)"),
            )

        nc.scalar.activation(out=rounded[:, S - P : S, :], in_=last_back[:].rearrange("p t j -> p j t"), func=SILU)
        groups = (slice(0, 2 * P), slice(2 * P, S - P))
        for cols in groups:
            round_result(cols)
        for cols in groups:
            quantize_result(cols)
        quantize_result(slice(S - P, S))
        nc.scalar.dma_start(out=code_view, in_=out_codes[:].bitcast(I32))
        for q in range(QUADS):
            queue = nc.scalar if q == QUADS - 1 else nc.sync
            queue.dma_start(
                out=out_2[0, 4 * q : 4 * q + 4, :].bitcast(I32),
                in_=out_bytes[32 * q : 32 * q + 4, :].bitcast(I32),
            )
